import numpy as np
import ml_dtypes


def mxq(x, axis, fmt="e4m3"):
    dtype, down = {"e4m3": (ml_dtypes.float8_e4m3fn, 7), "e5m2": (ml_dtypes.float8_e5m2, 14)}[fmt]
    v = np.moveaxis(np.asarray(x, np.float32).astype(ml_dtypes.bfloat16).astype(np.float64), axis, -1)
    blocks = v.reshape(v.shape[:-1] + (-1, 32))
    amax = np.abs(blocks).max(-1, keepdims=True)
    byte = np.maximum(np.where(amax > 0, np.frexp(amax)[1] - 1 + 127, 0) - down, 1)
    scale = np.exp2(byte - 127.0)
    codes = (blocks / scale).astype(np.float32).astype(dtype).astype(np.float64)
    return np.moveaxis((codes * scale).reshape(v.shape), -1, axis)


WIDE = False


def mx_kscale(k):
    if not WIDE:
        return np.ones(k)
    levels = np.array([10, -10, 5, -5, 0])
    if k % 512:
        return np.exp2(np.random.permutation(np.resize(levels, k // 32))).repeat(32)
    a = np.empty((k // 512, 16))
    for p in range(k // 512):
        a[p, :8] = np.random.permutation(np.resize(levels, 8))
        for g in range(8):
            far = levels[np.abs(levels - a[p, g]) >= 10]
            a[p, g + 8] = far[np.random.randint(len(far))]
    return np.exp2(a.ravel()).repeat(32)


def f64(x):
    return np.asarray(x).astype(np.float64)


def striped(idx):
    return np.tile(idx.reshape(-1, 16).T, (8, 1)).astype(np.uint16)


def unstriped(offs):
    return offs[:16].T.reshape(-1).astype(np.int64)


def striped8(idx):
    return np.concatenate([x.reshape(-1, 16).T for x in idx]).astype(np.uint16)


def runs(offs, k):
    lists = np.stack([offs[16 * r : 16 * r + 16].T.reshape(-1) for r in range(8)]).astype(np.int64)
    return lists[np.arange(k) % 512 // 64]


def pack_weight(w):
    k, n = w.shape
    w = f64(np.asarray(w, np.float32).astype(ml_dtypes.bfloat16)).reshape(k // 32, 32, n)
    amax = np.abs(w).max(1)
    byte = np.clip(np.where(amax > 0, np.frexp(amax)[1] - 1 + 127 - 7, 1), 1, 254)
    scaled = (w * np.exp2(127.0 - byte)[:, None, :]).reshape(k, n).astype(np.float32)
    words = np.ascontiguousarray(scaled.reshape(k // 512, 128, 4, n).transpose(0, 1, 3, 2)).astype(ml_dtypes.float8_e4m3fn).view(np.uint8)
    return words, np.ascontiguousarray(byte.astype(np.uint8).reshape(k // 512, 16, n))


def unpack_weight(words, scales):
    g, p, n, _ = words.shape
    vals = np.ascontiguousarray(words).view(ml_dtypes.float8_e4m3fn).astype(np.float64) * np.repeat(np.exp2(scales.astype(np.float64) - 127.0), 8, axis=1)[..., None]
    return vals.transpose(0, 1, 3, 2).reshape(g * 512, n)


E2M1 = np.array([0.0, 0.5, 1.0, 1.5, 2.0, 3.0, 4.0, 6.0, -0.0, -0.5, -1.0, -1.5, -2.0, -3.0, -4.0, -6.0])


def pack_fp4(w):
    k, n = w.shape
    w = f64(np.asarray(w, np.float32).astype(ml_dtypes.bfloat16)).reshape(k // 32, 32, n)
    amax = np.abs(w).max(1)
    mant, ex = np.frexp(amax / 6.0)
    byte = np.clip(np.where(amax > 0, np.where(mant > 0.5, ex, ex - 1) + 127, 1), 1, 254)
    scaled = (w * np.exp2(127.0 - byte)[:, None, :]).reshape(k, n).astype(np.float32)
    c = np.ascontiguousarray(scaled.reshape(k // 512, 128, 4, n).transpose(0, 1, 3, 2)).astype(ml_dtypes.float4_e2m1fn).view(np.uint8) & 0xF
    words = (c[..., 0::2] | (c[..., 1::2] << 4)).reshape(k // 512, 128, 2 * n)
    return np.ascontiguousarray(words), np.ascontiguousarray(byte.astype(np.uint8).reshape(k // 512, 16, n))


def unpack_fp4(words, scales):
    g, _, n = scales.shape
    words = np.ascontiguousarray(words).reshape(g, 128, n, 2)
    nib = np.empty((g, 128, n, 4), np.uint8)
    nib[..., 0::2] = words & 0xF
    nib[..., 1::2] = words >> 4
    vals = E2M1[nib] * np.repeat(np.exp2(scales.astype(np.float64) - 127.0), 8, axis=1)[..., None]
    return vals.transpose(0, 1, 3, 2).reshape(g * 512, n)


def sigmoid(v):
    return 1.0 / (1.0 + np.exp(-np.maximum(v, -700.0)))

def planes(y):
    n, m = y.shape
    v = y.astype(np.float32).astype(ml_dtypes.bfloat16).astype(np.float64).reshape(n // 32, 32, m)
    top = np.abs(v).max(1)
    byte = np.clip(np.where(top > 0, np.frexp(top)[1] - 1 + 127 - 7, 1), 1, 254)
    codes = (v * np.exp2(127.0 - byte)[:, None, :]).reshape(n, m).astype(np.float32).astype(ml_dtypes.float8_e4m3fn).view(np.uint8)
    words = codes.reshape(n // 512, 128, 4, m).transpose(0, 1, 3, 2)
    return np.ascontiguousarray(words), np.ascontiguousarray(byte.astype(np.uint8).reshape(n // 512, 16, m))


K, T, S, N, H = 512, 2048, 512, 512, 512


def setup_inputs():
    n = np.random.standard_normal
    s = mx_kscale(K)[:, None]
    u = mx_kscale(H)
    packed_xT = pack_weight(n((K, T)) * s)
    packed_w1 = pack_fp4(n((K, H)) / np.sqrt(K) / s)
    packed_w2 = pack_fp4(n((H, N)) / np.sqrt(H) / u[:, None])
    return {
        "x_words": packed_xT[0],
        "x_scales": packed_xT[1],
        "w1_words": packed_w1[0],
        "w1_scales": packed_w1[1],
        "gn": (np.random.uniform(0.5, 1.5, (H, 1)) * u[:, None]).astype(np.float32),
        "w2_words": packed_w2[0],
        "w2_scales": packed_w2[1],
        "offs": striped(np.random.permutation(T)[:S]),
        "p1": striped8(np.stack([np.random.permutation(S) for _ in range(8)])),
        "p2": striped8(np.stack([np.random.permutation(S) for _ in range(8)])),
        "p3": striped8(np.stack([np.random.permutation(S) for _ in range(8)])),
    }


def reference(x_words, x_scales, w1_words, w1_scales, gn, w2_words, w2_scales, offs, p1, p2, p3):
    xq = unpack_weight(x_words, x_scales)[:, unstriped(offs)]
    y = unpack_fp4(w1_words, w1_scales).T @ xq
    z = f64(gn) * (0.5 * (sigmoid(4.0 * (y[np.arange(H)[:, None], runs(p1, H)] - y)) + 2.0 * (sigmoid(4.0 * (y[np.arange(H)[:, None], runs(p2, H)] - y))) + 4.0 * (sigmoid(4.0 * (y[np.arange(H)[:, None], runs(p3, H)] - y)))) + -1.75)
    out_0 = unpack_fp4(w2_words, w2_scales).T @ mxq(z, 0, "e4m3")
    return (out_0,) + planes(out_0)

@@ -1,0 +1,233 @@
+from contextlib import ExitStack
+
+import concourse.mybir as mybir
+
+K, T, S, N, H = 512, 2048, 512, 512, 512
+FLOPS = 2 * K * H * S + 2 * H * N * S
+
+F32 = mybir.dt.float32
+BF16 = mybir.dt.bfloat16
+I32 = mybir.dt.int32
+U32 = mybir.dt.uint32
+U16 = mybir.dt.uint16
+U8 = mybir.dt.uint8
+FP8X4 = mybir.dt.float8_e4m3fn_x4
+FP4X4 = mybir.dt.float4_e2m1fn_x4
+ALU = mybir.AluOpType
+ACT = mybir.ActivationFunctionType
+
+P = 128
+PACK = 4
+QUADS = 4
+BLOCK = 128
+HALF = 256
+CHUNKS = [(0, 256), (256, 128), (384, 128)]
+
+
+def load_scale_rows(queues, tile, scales):
+    for q in range(QUADS):
+        queues[q].dma_start(out=tile[32 * q : 32 * q + 4, :].bitcast(I32), in_=scales[0, 4 * q : 4 * q + 4, :].bitcast(I32))
+
+
+def deal(nc, words, scales, raw_words, raw_scales, ts):
+    nc.vector.tensor_copy(
+        out=words[:].rearrange("p (t m b) -> p t m b", t=PACK, b=2)[:, ts],
+        in_=raw_words[:].rearrange("p (m t b) -> p t m b", t=PACK, b=2)[:, ts],
+    )
+    nc.vector.tensor_copy(
+        out=scales[:].rearrange("p (t m) -> p t m", t=PACK)[:, ts],
+        in_=raw_scales[:].rearrange("p (m t) -> p t m", t=PACK)[:, ts],
+    )
+
+
+def tile_picked_census8_none_po_kernel(
+    tc, x_words, x_scales, w1_words, w1_scales, gn, w2_words, w2_scales, offs, p1, p2, p3, out_0, out_1, out_2
+):
+    nc = tc.nc
+    with ExitStack() as ctx:
+        keep = ctx.enter_context(tc.tile_pool(name="keep", bufs=1))
+        ring = ctx.enter_context(tc.tile_pool(name="ring", bufs=3))
+        psum = ctx.enter_context(tc.psum_pool(name="psum", bufs=1))
+
+        def tile(name, shape, dtype):
+            return keep.tile(shape, dtype, name=name, align_bytes=64)
+
+        offs_sb = tile("offs_sb", [P, S // 16], U16)
+        lists = [tile("list%d" % k, [P, S // 16], U16) for k in range(3)]
+        xw = tile("xw", [P, T], U32)
+        xs = tile("xs", [P, T], U8)
+        ww_raw = tile("ww_raw", [P, 2 * H], U8)
+        ws_raw = tile("ws_raw", [P, H], U8)
+
+        warm = keep.tile([P, 2], F32, name="warm", tag="small", align_bytes=64)
+        nc.vector.memset(xs[:].bitcast(I32), 0)
+        nc.vector.memset(ws_raw[:].bitcast(I32), 0)
+        nc.vector.memset(warm[:, 0:1], 0.0)
+        nc.sync.dma_start(offs_sb[:], offs)
+        nc.sync.dma_start(out=xw[:].bitcast(I32), in_=x_words[0].rearrange("p n t -> p (n t)").bitcast(I32))
+        load_scale_rows([nc.scalar, nc.sync, nc.scalar, nc.sync], xs, x_scales)
+        nc.sync.dma_start(out=ww_raw[:].bitcast(I32), in_=w1_words[0].bitcast(I32))
+        for list_sb, list_in in zip(lists, (p1, p2, p3)):
+            nc.sync.dma_start(list_sb[:], list_in)
+        nc.scalar.activation(out=warm[:, 1:2], in_=warm[:, 0:1], func=ACT.Tanh)
+        load_scale_rows([nc.gpsimd, nc.gpsimd, nc.gpsimd, nc.scalar], ws_raw, w1_scales)
+        gain = keep.tile([P, PACK], F32, name="gain", tag="small", align_bytes=64)
+        nc.sync.dma_start(out=gain[:], in_=gn.rearrange("(p t) o -> p (t o)", t=PACK))
+
+
+        xs_p = tile("xs_p", [P, S], U8)
+        xw_p = tile("xw_p", [P, S], U32)
+        w1w = tile("w1w", [P, 2 * H], U8)
+        w1s = tile("w1s", [P, H], U8)
+        w2w = tile("w2w", [P, 2 * N], U8)
+        w2s = tile("w2s", [P, N], U8)
+        deal(nc, w1w, w1s, ww_raw, ws_raw, slice(0, 1))
+        for h in range(2):
+            cols = slice(h * HALF, (h + 1) * HALF)
+            entries = offs_sb[:, h * HALF // 16 : (h + 1) * HALF // 16]
+            nc.vector.tensor_copy(out=xs_p[:, cols], in_=xs[:].indirect(entries))
+            nc.vector.tensor_copy(out=xw_p[:, cols], in_=xw[:].indirect(entries))
+        deal(nc, w1w, w1s, ww_raw, ws_raw, slice(1, PACK))
+        nc.sync.dma_start(out=ww_raw[:].bitcast(I32), in_=w2_words[0].bitcast(I32))
+        load_scale_rows([nc.sync] * 4, ws_raw, w2_scales)
+        deal(nc, w2w, w2s, ww_raw, ws_raw, slice(0, PACK))
+
+        gain_quarter = tile("gain_quarter", [P, PACK], F32)
+        gain_half = tile("gain_half", [P, PACK], F32)
+        nc.gpsimd.tensor_scalar(gain_quarter[:], gain[:], 0.25, 0.0, ALU.mult, ALU.add)
+        nc.gpsimd.tensor_scalar(gain_half[:], gain[:], 0.5, 0.0, ALU.mult, ALU.add)
+
+        y_ps = [[psum.tile([P, HALF], F32, name="y_ps%d_%d" % (t, h), tag="bank%d" % (2 * t + h)) for h in range(2)] for t in range(PACK)]
+        y_win = [tile("y_win%d" % t, [P, S], F32) for t in range(PACK)]
+        y_own = [[tile("y_own%d_%d" % (t, h), [P, HALF], F32) for h in range(2)] for t in range(PACK)]
+        for t in range(PACK):
+            for h in range(2):
+                cols = slice(h * HALF, (h + 1) * HALF)
+                nc.tensor.matmul_mx(
+                    out=y_ps[t][h][:],
+                    lhsT=w1w[:, 2 * P * t : 2 * P * (t + 1)].bitcast(FP4X4),
+                    lhsT_scale=w1s[:, P * t : P * (t + 1)],
+                    rhs=xw_p[:, cols].bitcast(FP8X4),
+                    rhs_scale=xs_p[:, cols],
+                    start=True,
+                    stop=True,
+                )
+
+        def fetch_y(t):
+            nc.scalar.copy(out=y_win[t][:, :HALF], in_=y_ps[t][0][:])
+            nc.scalar.copy(out=y_own[t][0][:], in_=y_ps[t][0][:])
+            nc.scalar.copy(out=y_win[t][:, HALF:], in_=y_ps[t][1][:])
+
+        def fetch_own(t):
+            nc.scalar.copy(out=y_own[t][1][:], in_=y_ps[t][1][:])
+
+        zw = tile("zw", [P, S], U32)
+        zs = tile("zs", [P, S], U8)
+        ow = tile("ow", [P, S], U32)
+        osc = tile("osc", [P, S], U8)
+        out_rows = out_0.rearrange("(p t) j -> p t j", t=PACK)
+        out_words = out_1[0].rearrange("p n t -> p (n t)").bitcast(I32)
+
+        z_rows = [tile("z_rows%d" % c, [P, PACK, n], BF16) for c, (lo, n) in enumerate(CHUNKS)]
+        partial = {}
+
+        def compare(c, ts, k):
+            lo, n = CHUNKS[c]
+            tag = "%d_%d_%d" % (c, ts[0], k)
+            diff = ring.tile([P, len(ts), n], F32, name="diff")
+            th = tile("th" + tag, [P, len(ts), n], F32)
+            for i, t in enumerate(ts):
+                nc.vector.tensor_tensor(
+                    diff[:, i, :],
+                    y_win[t][:].indirect(lists[k][:, lo // 16 : (lo + n) // 16]),
+                    y_own[t][lo // HALF][:, lo % HALF : lo % HALF + n],
+                    ALU.subtract,
+                )
+            nc.scalar.activation(out=th[:], in_=diff[:], func=ACT.Tanh, scale=2.0)
+            for i, t in enumerate(ts):
+                if k == 0:
+                    partial[c, t] = tile("first%d_%d" % (c, t), [P, n], F32)
+                    nc.scalar.activation(out=partial[c, t][:], in_=th[:, i, :], func=ACT.Copy, scale=gain_quarter[:, t : t + 1])
+                elif k == 1:
+                    second = tile("second%d_%d" % (c, t), [P, n], F32)
+                    nc.vector.scalar_tensor_tensor(second[:], th[:, i, :], gain_half[:, t : t + 1], partial[c, t][:], ALU.mult, ALU.add)
+                    partial[c, t] = second
+                else:
+                    nc.vector.scalar_tensor_tensor(z_rows[c][:, t, :], th[:, i, :], gain[:, t : t + 1], partial[c, t][:], ALU.mult, ALU.add)
+
+        def census(c, ts):
+            for k in range(3):
+                compare(c, ts, k)
+
+        o_ps = {}
+
+        def layer(b, copy):
+            cols = slice(b * BLOCK, (b + 1) * BLOCK)
+            c = [lo <= cols.start < lo + n for lo, n in CHUNKS].index(True)
+            lo = CHUNKS[c][0]
+            z16 = tile("z16_%d" % b, [P, BLOCK, PACK], BF16)
+            copy(out=z16[:], in_=z_rows[c][:, :, cols.start - lo : cols.stop - lo].rearrange("p t n -> p n t"))
+            nc.vector.quantize_mx(out=zw[:, cols].bitcast(FP8X4), scales=zs[:, cols], in_=z16[:].rearrange("p n t -> p (n t)"))
+            o_ps[b] = psum.tile([P, PACK, BLOCK], F32, name="o_ps%d" % b, tag="bank%d" % b)
+            for t in range(PACK):
+                nc.tensor.matmul_mx(
+                    out=o_ps[b][:, t, :],
+                    lhsT=w2w[:, 2 * P * t : 2 * P * (t + 1)].bitcast(FP4X4),
+                    lhsT_scale=w2s[:, P * t : P * (t + 1)],
+                    rhs=zw[:, cols].bitcast(FP8X4),
+                    rhs_scale=zs[:, cols],
+                    start=True,
+                    stop=True,
+                )
+
+        def planes(b, copy):
+            cols = slice(b * BLOCK, (b + 1) * BLOCK)
+            o16 = tile("o16_%d" % b, [P, BLOCK, PACK], BF16)
+            copy(out=o16[:], in_=o_ps[b][:].rearrange("p t n -> p n t"))
+            nc.vector.quantize_mx(out=ow[:, cols].bitcast(FP8X4), scales=osc[:, cols], in_=o16[:].rearrange("p n t -> p (n t)"))
+            nc.sync.dma_start(out=out_words[:, cols], in_=ow[:, cols].bitcast(I32))
+
+        def result(b, queue):
+            cols = slice(b * BLOCK, (b + 1) * BLOCK)
+            o32 = tile("o32_%d" % b, [P, PACK, BLOCK], F32)
+            nc.scalar.copy(out=o32[:], in_=o_ps[b][:])
+            queue.dma_start(out=out_rows[:, :, cols], in_=o32[:])
+
+        fetch_y(0)
+        fetch_y(1)
+        census(0, [0])
+        fetch_y(2)
+        census(0, [1])
+        fetch_y(3)
+        fetch_own(0)
+        fetch_own(1)
+        census(0, [2])
+        fetch_own(2)
+        fetch_own(3)
+        census(0, [3])
+        compare(1, [0, 1], 0)
+        layer(0, nc.scalar.copy)
+        compare(1, [0, 1], 1)
+        compare(1, [0, 1], 2)
+        layer(1, nc.scalar.copy)
+        compare(1, [2, 3], 0)
+        compare(1, [2, 3], 1)
+        planes(0, nc.scalar.copy)
+        compare(1, [2, 3], 2)
+        result(0, nc.sync)
+        compare(2, [0, 1], 0)
+        layer(2, nc.scalar.copy)
+        compare(2, [0, 1], 1)
+        planes(1, nc.scalar.copy)
+        compare(2, [0, 1], 2)
+        result(1, nc.sync)
+        compare(2, [2, 3], 0)
+        compare(2, [2, 3], 1)
+        compare(2, [2, 3], 2)
+        planes(2, nc.scalar.copy)
+        result(2, nc.sync)
+        layer(3, nc.vector.tensor_copy)
+        planes(3, nc.scalar.copy)
+        result(3, nc.scalar)
+        for q in range(QUADS):
+            (nc.sync if q < 2 else nc.scalar).dma_start(out=out_2[0, 4 * q : 4 * q + 4, :].bitcast(I32), in_=osc[32 * q : 32 * q + 4, :].bitcast(I32))

@@ -29,14 +29,17 @@ def load_scale_rows(queues, tile, scales):
         queues[q].dma_start(out=tile[32 * q : 32 * q + 4, :].bitcast(I32), in_=scales[0, 4 * q : 4 * q + 4, :].bitcast(I32))
 
 
-def deal(nc, words, scales, raw_words, raw_scales, ts):
-    nc.vector.tensor_copy(
-        out=words[:].rearrange("p (t m b) -> p t m b", t=PACK, b=2)[:, ts],
-        in_=raw_words[:].rearrange("p (m t b) -> p t m b", t=PACK, b=2)[:, ts],
+def deal_words(engine, words, raw_words):
+    engine.tensor_copy(
+        out=words[:].rearrange("p (t c m b) -> p c t m b", t=PACK, m=8, b=2),
+        in_=raw_words[:].rearrange("p (c m t b) -> p c t m b", t=PACK, m=8, b=2),
     )
-    nc.vector.tensor_copy(
-        out=scales[:].rearrange("p (t m) -> p t m", t=PACK)[:, ts],
-        in_=raw_scales[:].rearrange("p (m t) -> p t m", t=PACK)[:, ts],
+
+
+def deal_scales(engine, scales, raw_scales, ts=slice(0, PACK)):
+    engine.tensor_copy(
+        out=scales[:].rearrange("p (t c m) -> p c t m", t=PACK, m=16)[:, :, ts],
+        in_=raw_scales[:].rearrange("p (c m t) -> p c t m", t=PACK, m=16)[:, :, ts],
     )
 
 
@@ -56,41 +59,48 @@ def tile_picked_census8_none_po_kernel(
         lists = [tile("list%d" % k, [P, S // 16], U16) for k in range(3)]
         xw = tile("xw", [P, T], U32)
         xs = tile("xs", [P, T], U8)
-        ww_raw = tile("ww_raw", [P, 2 * H], U8)
-        ws_raw = tile("ws_raw", [P, H], U8)
+        w1w_raw = tile("w1w_raw", [P, 2 * H], U8)
+        w1s_raw = tile("w1s_raw", [P, H], U8)
+        w2w_raw = tile("w2w_raw", [P, 2 * N], U8)
+        w2s_raw = tile("w2s_raw", [P, N], U8)
+        gain = tile("gain", [P, PACK], F32)
 
-        warm = keep.tile([P, 2], F32, name="warm", tag="small", align_bytes=64)
-        nc.vector.memset(xs[:].bitcast(I32), 0)
-        nc.vector.memset(ws_raw[:].bitcast(I32), 0)
+        warm = tile("warm", [P, 2], F32)
+        nc.vector.memset(w1s_raw[:].bitcast(I32), 0)
+        nc.vector.memset(xs[:, :1280].bitcast(I32), 0)
+        nc.gpsimd.memset(xs[:, 1280:].bitcast(I32), 0)
         nc.vector.memset(warm[:, 0:1], 0.0)
+        nc.vector.memset(w2s_raw[:].bitcast(I32), 0)
         nc.sync.dma_start(offs_sb[:], offs)
-        nc.sync.dma_start(out=xw[:].bitcast(I32), in_=x_words[0].rearrange("p n t -> p (n t)").bitcast(I32))
+        nc.sync.dma_start(lists[0][:], p1)
+        nc.sync.dma_start(out=w1w_raw[:].bitcast(I32), in_=w1_words[0].bitcast(I32))
+        nc.sync.dma_start(out=xw[:, 0:1216].bitcast(I32), in_=x_words[0, :, 0:1216, :].rearrange("p n t -> p (n t)").bitcast(I32))
         load_scale_rows([nc.scalar, nc.sync, nc.scalar, nc.sync], xs, x_scales)
-        nc.sync.dma_start(out=ww_raw[:].bitcast(I32), in_=w1_words[0].bitcast(I32))
-        for list_sb, list_in in zip(lists, (p1, p2, p3)):
-            nc.sync.dma_start(list_sb[:], list_in)
+        nc.sync.dma_start(out=xw[:, 1216:2048].bitcast(I32), in_=x_words[0, :, 1216:2048, :].rearrange("p n t -> p (n t)").bitcast(I32))
+        load_scale_rows([nc.gpsimd, nc.gpsimd, nc.sync, nc.sync], w1s_raw, w1_scales)
         nc.scalar.activation(out=warm[:, 1:2], in_=warm[:, 0:1], func=ACT.Tanh)
-        load_scale_rows([nc.gpsimd, nc.gpsimd, nc.gpsimd, nc.scalar], ws_raw, w1_scales)
-        gain = keep.tile([P, PACK], F32, name="gain", tag="small", align_bytes=64)
+        nc.sync.dma_start(lists[1][:], p2)
+        nc.sync.dma_start(out=w2w_raw[:].bitcast(I32), in_=w2_words[0].bitcast(I32))
+        nc.sync.dma_start(lists[2][:], p3)
         nc.sync.dma_start(out=gain[:], in_=gn.rearrange("(p t) o -> p (t o)", t=PACK))
+        load_scale_rows([nc.sync] * 4, w2s_raw, w2_scales)
 
 
         xs_p = tile("xs_p", [P, S], U8)
-        xw_p = tile("xw_p", [P, S], U32)
+        xw_p = [tile("xw_p%d" % h, [P, HALF], U32) for h in range(2)]
         w1w = tile("w1w", [P, 2 * H], U8)
         w1s = tile("w1s", [P, H], U8)
         w2w = tile("w2w", [P, 2 * N], U8)
         w2s = tile("w2s", [P, N], U8)
-        deal(nc, w1w, w1s, ww_raw, ws_raw, slice(0, 1))
+        nc.vector.tensor_copy(out=xs_p[:], in_=xs[:].indirect(offs_sb[:]))
+        deal_words(nc.vector, w1w, w1w_raw)
+        deal_scales(nc.gpsimd, w1s, w1s_raw, slice(0, 1))
+        deal_scales(nc.gpsimd, w1s, w1s_raw, slice(1, PACK))
         for h in range(2):
-            cols = slice(h * HALF, (h + 1) * HALF)
             entries = offs_sb[:, h * HALF // 16 : (h + 1) * HALF // 16]
-            nc.vector.tensor_copy(out=xs_p[:, cols], in_=xs[:].indirect(entries))
-            nc.vector.tensor_copy(out=xw_p[:, cols], in_=xw[:].indirect(entries))
-        deal(nc, w1w, w1s, ww_raw, ws_raw, slice(1, PACK))
-        nc.sync.dma_start(out=ww_raw[:].bitcast(I32), in_=w2_words[0].bitcast(I32))
-        load_scale_rows([nc.sync] * 4, ws_raw, w2_scales)
-        deal(nc, w2w, w2s, ww_raw, ws_raw, slice(0, PACK))
+            nc.vector.tensor_copy(out=xw_p[h][:], in_=xw[:].indirect(entries))
+        deal_words(nc.vector, w2w, w2w_raw)
+        deal_scales(nc.gpsimd, w2s, w2s_raw)
 
         gain_quarter = tile("gain_quarter", [P, PACK], F32)
         gain_half = tile("gain_half", [P, PACK], F32)
@@ -107,7 +117,7 @@ def tile_picked_census8_none_po_kernel(
                     out=y_ps[t][h][:],
                     lhsT=w1w[:, 2 * P * t : 2 * P * (t + 1)].bitcast(FP4X4),
                     lhsT_scale=w1s[:, P * t : P * (t + 1)],
-                    rhs=xw_p[:, cols].bitcast(FP8X4),
+                    rhs=xw_p[h][:].bitcast(FP8X4),
                     rhs_scale=xs_p[:, cols],
                     start=True,
                     stop=True,

@@ -60,25 +60,21 @@ def tile_picked_census8_none_po_kernel(
         xw = tile("xw", [P, T], U32)
         xs = tile("xs", [P, T], U8)
         w1w_raw = tile("w1w_raw", [P, 2 * H], U8)
-        w1s_raw = tile("w1s_raw", [P, H], U8)
+        w1s_raw = keep.tile([P, H], U8, name="w1s_raw", tag="w1s_then_x", align_bytes=64)
         w2w_raw = tile("w2w_raw", [P, 2 * N], U8)
         w2s_raw = tile("w2s_raw", [P, N], U8)
         gain = tile("gain", [P, PACK], F32)
 
-        warm = tile("warm", [P, 2], F32)
+        nc.vector.memset(xs[:, :1152].bitcast(I32), 0)
+        nc.gpsimd.memset(xs[:, 1152:].bitcast(I32), 0)
         nc.vector.memset(w1s_raw[:].bitcast(I32), 0)
-        nc.vector.memset(xs[:, :1280].bitcast(I32), 0)
-        nc.gpsimd.memset(xs[:, 1280:].bitcast(I32), 0)
-        nc.vector.memset(warm[:, 0:1], 0.0)
-        nc.vector.memset(w2s_raw[:].bitcast(I32), 0)
+        nc.gpsimd.memset(w2s_raw[:].bitcast(I32), 0)
         nc.sync.dma_start(offs_sb[:], offs)
         nc.sync.dma_start(lists[0][:], p1)
         nc.sync.dma_start(out=w1w_raw[:].bitcast(I32), in_=w1_words[0].bitcast(I32))
-        nc.sync.dma_start(out=xw[:, 0:1216].bitcast(I32), in_=x_words[0, :, 0:1216, :].rearrange("p n t -> p (n t)").bitcast(I32))
         load_scale_rows([nc.scalar, nc.sync, nc.scalar, nc.sync], xs, x_scales)
-        nc.sync.dma_start(out=xw[:, 1216:2048].bitcast(I32), in_=x_words[0, :, 1216:2048, :].rearrange("p n t -> p (n t)").bitcast(I32))
-        load_scale_rows([nc.gpsimd, nc.gpsimd, nc.sync, nc.sync], w1s_raw, w1_scales)
-        nc.scalar.activation(out=warm[:, 1:2], in_=warm[:, 0:1], func=ACT.Tanh)
+        nc.sync.dma_start(out=xw[:].bitcast(I32), in_=x_words[0].rearrange("p n t -> p (n t)").bitcast(I32))
+        load_scale_rows([nc.sync] * 4, w1s_raw, w1_scales)
         nc.sync.dma_start(lists[1][:], p2)
         nc.sync.dma_start(out=w2w_raw[:].bitcast(I32), in_=w2_words[0].bitcast(I32))
         nc.sync.dma_start(lists[2][:], p3)
@@ -87,25 +83,22 @@ def tile_picked_census8_none_po_kernel(
 
 
         xs_p = tile("xs_p", [P, S], U8)
-        xw_p = [tile("xw_p%d" % h, [P, HALF], U32) for h in range(2)]
+        xw_p = [tile("xw_p0", [P, HALF], U32), keep.tile([P, HALF], U32, name="xw_p1", tag="w1s_then_x", align_bytes=64)]
         w1w = tile("w1w", [P, 2 * H], U8)
         w1s = tile("w1s", [P, H], U8)
         w2w = tile("w2w", [P, 2 * N], U8)
         w2s = tile("w2s", [P, N], U8)
         nc.vector.tensor_copy(out=xs_p[:], in_=xs[:].indirect(offs_sb[:]))
         deal_words(nc.vector, w1w, w1w_raw)
-        deal_scales(nc.gpsimd, w1s, w1s_raw, slice(0, 1))
-        deal_scales(nc.gpsimd, w1s, w1s_raw, slice(1, PACK))
+        deal_scales(nc.vector, w1s, w1s_raw)
         for h in range(2):
             entries = offs_sb[:, h * HALF // 16 : (h + 1) * HALF // 16]
             nc.vector.tensor_copy(out=xw_p[h][:], in_=xw[:].indirect(entries))
         deal_words(nc.vector, w2w, w2w_raw)
-        deal_scales(nc.gpsimd, w2s, w2s_raw)
+        deal_scales(nc.vector, w2s, w2s_raw)
 
         gain_quarter = tile("gain_quarter", [P, PACK], F32)
         gain_half = tile("gain_half", [P, PACK], F32)
-        nc.gpsimd.tensor_scalar(gain_quarter[:], gain[:], 0.25, 0.0, ALU.mult, ALU.add)
-        nc.gpsimd.tensor_scalar(gain_half[:], gain[:], 0.5, 0.0, ALU.mult, ALU.add)
 
         y_ps = [[psum.tile([P, HALF], F32, name="y_ps%d_%d" % (t, h), tag="bank%d" % (2 * t + h)) for h in range(2)] for t in range(PACK)]
         y_win = [tile("y_win%d" % t, [P, S], F32) for t in range(PACK)]
@@ -133,7 +126,6 @@ def tile_picked_census8_none_po_kernel(
 
         zw = tile("zw", [P, S], U32)
         zs = tile("zs", [P, S], U8)
-        ow = tile("ow", [P, S], U32)
         osc = tile("osc", [P, S], U8)
         out_rows = out_0.rearrange("(p t) j -> p t j", t=PACK)
         out_words = out_1[0].rearrange("p n t -> p (n t)").bitcast(I32)
@@ -190,21 +182,57 @@ def tile_picked_census8_none_po_kernel(
                     stop=True,
                 )
 
-        def planes(b, copy):
-            cols = slice(b * BLOCK, (b + 1) * BLOCK)
-            o16 = tile("o16_%d" % b, [P, BLOCK, PACK], BF16)
-            copy(out=o16[:], in_=o_ps[b][:].rearrange("p t n -> p n t"))
-            nc.vector.quantize_mx(out=ow[:, cols].bitcast(FP8X4), scales=osc[:, cols], in_=o16[:].rearrange("p n t -> p (n t)"))
-            nc.sync.dma_start(out=out_words[:, cols], in_=ow[:, cols].bitcast(I32))
+        o16 = tile("o16", [P, S - BLOCK, PACK], BF16)
 
-        def result(b, queue):
-            cols = slice(b * BLOCK, (b + 1) * BLOCK)
-            o32 = tile("o32_%d" % b, [P, PACK, BLOCK], F32)
-            nc.scalar.copy(out=o32[:], in_=o_ps[b][:])
-            queue.dma_start(out=out_rows[:, :, cols], in_=o32[:])
+        def round_result(b):
+            nc.scalar.copy(out=o16[:, b * BLOCK : (b + 1) * BLOCK, :], in_=o_ps[b][:].rearrange("p t n -> p n t"))
+
+        o32_chunk = [tile("o32_%d" % c, [P, PACK, n], F32) for c, (lo, n) in enumerate(CHUNKS[:2])]
+
+        def result(b):
+            c = b // 2
+            lo, n = CHUNKS[c]
+            nc.scalar.copy(out=o32_chunk[c][:, :, b * BLOCK - lo : (b + 1) * BLOCK - lo], in_=o_ps[b][:])
+            if (b + 1) * BLOCK == lo + n:
+                nc.sync.dma_start(out=out_rows[:, :, lo : lo + n], in_=o32_chunk[c][:])
+
+        def early_planes():
+            ow_early = keep.tile([P, S - BLOCK], U32, name="ow_early", tag="late", align_bytes=64)
+            for cols in (slice(0, 2 * BLOCK), slice(2 * BLOCK, 3 * BLOCK)):
+                nc.vector.quantize_mx(out=ow_early[:, cols].bitcast(FP8X4), scales=osc[:, cols], in_=o16[:, cols, :].rearrange("p n t -> p (n t)"))
+            nc.sync.dma_start(out=out_words[:, : S - BLOCK], in_=ow_early[:].bitcast(I32))
+
+        def last_block():
+            cols = slice(S - BLOCK, S)
+            z16 = keep.tile([P, BLOCK, PACK], BF16, name="z16_last", tag="late", align_bytes=64)
+            nc.vector.tensor_copy(out=z16[:], in_=z_rows[2][:].rearrange("p t n -> p n t"))
+            nc.vector.quantize_mx(out=zw[:, cols].bitcast(FP8X4), scales=zs[:, cols], in_=z16[:].rearrange("p n t -> p (n t)"))
+            pairs = [psum.tile([P, 2, BLOCK], F32, name="o_last%d" % u, tag="bank%d" % (3 + u)) for u in range(2)]
+            for t in range(PACK):
+                nc.tensor.matmul_mx(
+                    out=pairs[t // 2][:, t % 2, :],
+                    lhsT=w2w[:, 2 * P * t : 2 * P * (t + 1)].bitcast(FP4X4),
+                    lhsT_scale=w2s[:, P * t : P * (t + 1)],
+                    rhs=zw[:, cols].bitcast(FP8X4),
+                    rhs_scale=zs[:, cols],
+                    start=True,
+                    stop=True,
+                )
+            early_planes()
+            o32 = tile("o32_last", [P, PACK, BLOCK], F32)
+            nc.scalar.copy(out=o32[:, 0:2, :], in_=pairs[0][:])
+            nc.vector.tensor_copy(out=o32[:, 2:4, :], in_=pairs[1][:])
+            nc.scalar.dma_start(out=out_rows[:, :, cols], in_=o32[:])
+            o16_last = tile("o16_last", [P, BLOCK, PACK], BF16)
+            ow_last = tile("ow_last", [P, BLOCK], U32)
+            nc.vector.tensor_copy(out=o16_last[:], in_=o32[:].rearrange("p t n -> p n t"))
+            nc.vector.quantize_mx(out=ow_last[:].bitcast(FP8X4), scales=osc[:, cols], in_=o16_last[:].rearrange("p n t -> p (n t)"))
+            nc.sync.dma_start(out=out_words[:, cols], in_=ow_last[:].bitcast(I32))
 
         fetch_y(0)
         fetch_y(1)
+        nc.scalar.activation(out=gain_quarter[:], in_=gain[:], func=ACT.Copy, scale=0.25)
+        nc.scalar.activation(out=gain_half[:], in_=gain[:], func=ACT.Copy, scale=0.5)
         census(0, [0])
         fetch_y(2)
         census(0, [1])
@@ -215,29 +243,22 @@ def tile_picked_census8_none_po_kernel(
         fetch_own(2)
         fetch_own(3)
         census(0, [3])
-        compare(1, [0, 1], 0)
         layer(0, nc.scalar.copy)
-        compare(1, [0, 1], 1)
-        compare(1, [0, 1], 2)
         layer(1, nc.scalar.copy)
-        compare(1, [2, 3], 0)
-        compare(1, [2, 3], 1)
-        planes(0, nc.scalar.copy)
-        compare(1, [2, 3], 2)
-        result(0, nc.sync)
-        compare(2, [0, 1], 0)
+        census(1, [0, 1])
+        result(0)
+        result(1)
+        census(1, [2, 3])
         layer(2, nc.scalar.copy)
-        compare(2, [0, 1], 1)
-        planes(1, nc.scalar.copy)
-        compare(2, [0, 1], 2)
-        result(1, nc.sync)
+        census(2, [0, 1])
         compare(2, [2, 3], 0)
         compare(2, [2, 3], 1)
-        compare(2, [2, 3], 2)
-        planes(2, nc.scalar.copy)
-        result(2, nc.sync)
-        layer(3, nc.vector.tensor_copy)
-        planes(3, nc.scalar.copy)
-        result(3, nc.scalar)
+        compare(2, [2], 2)
+        compare(2, [3], 2)
+        result(2)
+        round_result(0)
+        round_result(1)
+        round_result(2)
+        last_block()
         for q in range(QUADS):
             (nc.sync if q < 2 else nc.scalar).dma_start(out=out_2[0, 4 * q : 4 * q + 4, :].bitcast(I32), in_=osc[32 * q : 32 * q + 4, :].bitcast(I32))

@@ -19,9 +19,14 @@ ACT = mybir.ActivationFunctionType
 P = 128
 PACK = 4
 QUADS = 4
+GROUP = 16
+HALF = S // 2
 BLOCK = 128
-HALF = 256
-CHUNKS = [(0, 256), (256, 128), (384, 128)]
+LAST = S // BLOCK - 1
+XS_CLEAR_SPLIT = 1152
+DIFF_BUFS = 3
+NARROW_SLOTS = [0, 1]
+WIDE_SLOTS = [2, 3]
 
 
 def load_scale_rows(queues, tile, scales):
@@ -29,18 +34,38 @@ def load_scale_rows(queues, tile, scales):
         queues[q].dma_start(out=tile[32 * q : 32 * q + 4, :].bitcast(I32), in_=scales[0, 4 * q : 4 * q + 4, :].bitcast(I32))
 
 
-def deal_words(engine, words, raw_words):
-    engine.tensor_copy(
+def deal_words(nc, words, raw_words):
+    nc.vector.tensor_copy(
         out=words[:].rearrange("p (t c m b) -> p c t m b", t=PACK, m=8, b=2),
         in_=raw_words[:].rearrange("p (c m t b) -> p c t m b", t=PACK, m=8, b=2),
     )
 
 
-def deal_scales(engine, scales, raw_scales, ts=slice(0, PACK)):
-    engine.tensor_copy(
-        out=scales[:].rearrange("p (t c m) -> p c t m", t=PACK, m=16)[:, :, ts],
-        in_=raw_scales[:].rearrange("p (c m t) -> p c t m", t=PACK, m=16)[:, :, ts],
+def deal_scales(nc, scales, raw_scales):
+    nc.vector.tensor_copy(
+        out=scales[:].rearrange("p (t c m) -> p c t m", t=PACK, m=16),
+        in_=raw_scales[:].rearrange("p (c m t) -> p c t m", t=PACK, m=16),
     )
+
+
+def product(nc, out, words, scales, t, moving_words, moving_scales):
+    nc.tensor.matmul_mx(
+        out=out,
+        lhsT=words[:, 2 * P * t : 2 * P * (t + 1)].bitcast(FP4X4),
+        lhsT_scale=scales[:, P * t : P * (t + 1)],
+        rhs=moving_words.bitcast(FP8X4),
+        rhs_scale=moving_scales,
+        start=True,
+        stop=True,
+    )
+
+
+def quantise(nc, words, scales, interleaved):
+    nc.vector.quantize_mx(out=words.bitcast(FP8X4), scales=scales, in_=interleaved.rearrange("p n t -> p (n t)"))
+
+
+def block_columns(b):
+    return slice(b * BLOCK, (b + 1) * BLOCK)
 
 
 def tile_picked_census8_none_po_kernel(
@@ -49,216 +74,174 @@ def tile_picked_census8_none_po_kernel(
     nc = tc.nc
     with ExitStack() as ctx:
         keep = ctx.enter_context(tc.tile_pool(name="keep", bufs=1))
-        ring = ctx.enter_context(tc.tile_pool(name="ring", bufs=3))
+        ring = ctx.enter_context(tc.tile_pool(name="ring", bufs=DIFF_BUFS))
         psum = ctx.enter_context(tc.psum_pool(name="psum", bufs=1))
 
-        def tile(name, shape, dtype):
-            return keep.tile(shape, dtype, name=name, align_bytes=64)
+        def tile(name, shape, dtype, tag=None):
+            return keep.tile(shape, dtype, name=name, tag=tag or name, align_bytes=64)
 
-        offs_sb = tile("offs_sb", [P, S // 16], U16)
-        lists = [tile("list%d" % k, [P, S // 16], U16) for k in range(3)]
+        offs_sb = tile("offs_sb", [P, S // GROUP], U16)
+        lists = [tile("list%d" % k, [P, S // GROUP], U16) for k in range(3)]
         xw = tile("xw", [P, T], U32)
         xs = tile("xs", [P, T], U8)
         w1w_raw = tile("w1w_raw", [P, 2 * H], U8)
-        w1s_raw = keep.tile([P, H], U8, name="w1s_raw", tag="w1s_then_x", align_bytes=64)
+        w1s_raw = tile("w1s_raw", [P, H], U8, tag="w1_scales_then_picked_words")
         w2w_raw = tile("w2w_raw", [P, 2 * N], U8)
         w2s_raw = tile("w2s_raw", [P, N], U8)
         gain = tile("gain", [P, PACK], F32)
 
-        nc.vector.memset(xs[:, :1152].bitcast(I32), 0)
-        nc.gpsimd.memset(xs[:, 1152:].bitcast(I32), 0)
+        nc.vector.memset(xs[:, :XS_CLEAR_SPLIT].bitcast(I32), 0)
+        nc.gpsimd.memset(xs[:, XS_CLEAR_SPLIT:].bitcast(I32), 0)
         nc.vector.memset(w1s_raw[:].bitcast(I32), 0)
         nc.gpsimd.memset(w2s_raw[:].bitcast(I32), 0)
+
         nc.sync.dma_start(offs_sb[:], offs)
         nc.sync.dma_start(lists[0][:], p1)
         nc.sync.dma_start(out=w1w_raw[:].bitcast(I32), in_=w1_words[0].bitcast(I32))
         load_scale_rows([nc.scalar, nc.sync, nc.scalar, nc.sync], xs, x_scales)
         nc.sync.dma_start(out=xw[:].bitcast(I32), in_=x_words[0].rearrange("p n t -> p (n t)").bitcast(I32))
-        load_scale_rows([nc.sync] * 4, w1s_raw, w1_scales)
+        load_scale_rows([nc.sync] * QUADS, w1s_raw, w1_scales)
         nc.sync.dma_start(lists[1][:], p2)
         nc.sync.dma_start(out=w2w_raw[:].bitcast(I32), in_=w2_words[0].bitcast(I32))
         nc.sync.dma_start(lists[2][:], p3)
         nc.sync.dma_start(out=gain[:], in_=gn.rearrange("(p t) o -> p (t o)", t=PACK))
-        load_scale_rows([nc.sync] * 4, w2s_raw, w2_scales)
+        load_scale_rows([nc.sync] * QUADS, w2s_raw, w2_scales)
 
-
-        xs_p = tile("xs_p", [P, S], U8)
-        xw_p = [tile("xw_p0", [P, HALF], U32), keep.tile([P, HALF], U32, name="xw_p1", tag="w1s_then_x", align_bytes=64)]
+        xs_picked = tile("xs_picked", [P, S], U8)
+        xw_picked = [tile("xw_picked0", [P, HALF], U32), tile("xw_picked1", [P, HALF], U32, tag="w1_scales_then_picked_words")]
         w1w = tile("w1w", [P, 2 * H], U8)
         w1s = tile("w1s", [P, H], U8)
         w2w = tile("w2w", [P, 2 * N], U8)
         w2s = tile("w2s", [P, N], U8)
-        nc.vector.tensor_copy(out=xs_p[:], in_=xs[:].indirect(offs_sb[:]))
-        deal_words(nc.vector, w1w, w1w_raw)
-        deal_scales(nc.vector, w1s, w1s_raw)
+        nc.vector.tensor_copy(out=xs_picked[:], in_=xs[:].indirect(offs_sb[:]))
+        deal_words(nc, w1w, w1w_raw)
+        deal_scales(nc, w1s, w1s_raw)
         for h in range(2):
-            entries = offs_sb[:, h * HALF // 16 : (h + 1) * HALF // 16]
-            nc.vector.tensor_copy(out=xw_p[h][:], in_=xw[:].indirect(entries))
-        deal_words(nc.vector, w2w, w2w_raw)
-        deal_scales(nc.vector, w2s, w2s_raw)
+            entries = offs_sb[:, h * HALF // GROUP : (h + 1) * HALF // GROUP]
+            nc.vector.tensor_copy(out=xw_picked[h][:], in_=xw[:].indirect(entries))
+        deal_words(nc, w2w, w2w_raw)
+        deal_scales(nc, w2s, w2s_raw)
+
+        y_ps = [[psum.tile([P, HALF], F32, name="y_ps%d_%d" % (t, h), tag="bank%d" % (2 * t + h)) for h in range(2)] for t in range(PACK)]
+        y_window = [tile("y_window%d" % t, [P, 2 * S if t in WIDE_SLOTS else S], F32) for t in range(PACK)]
+        y_own = [tile("y_own%d" % t, [P, S], F32) for t in range(PACK)]
+        for t in WIDE_SLOTS:
+            nc.vector.memset(y_window[t][:, S:], 0.0)
+        for t in range(PACK):
+            for h in range(2):
+                product(nc, y_ps[t][h][:], w1w, w1s, t, xw_picked[h][:], xs_picked[:, h * HALF : (h + 1) * HALF])
+
+        def fetch_window(t):
+            nc.scalar.copy(out=y_window[t][:, :HALF], in_=y_ps[t][0][:])
+            nc.scalar.copy(out=y_own[t][:, :HALF], in_=y_ps[t][0][:])
+            nc.scalar.copy(out=y_window[t][:, HALF:S], in_=y_ps[t][1][:])
+
+        def fetch_second_half(t):
+            nc.scalar.copy(out=y_own[t][:, HALF:], in_=y_ps[t][1][:])
 
         gain_quarter = tile("gain_quarter", [P, PACK], F32)
         gain_half = tile("gain_half", [P, PACK], F32)
+        z_slots = tile("z_slots", [P, PACK, S], BF16)
+        partial = {}
 
-        y_ps = [[psum.tile([P, HALF], F32, name="y_ps%d_%d" % (t, h), tag="bank%d" % (2 * t + h)) for h in range(2)] for t in range(PACK)]
-        y_win = [tile("y_win%d" % t, [P, S], F32) for t in range(PACK)]
-        y_own = [[tile("y_own%d_%d" % (t, h), [P, HALF], F32) for h in range(2)] for t in range(PACK)]
-        for t in range(PACK):
-            for h in range(2):
-                cols = slice(h * HALF, (h + 1) * HALF)
-                nc.tensor.matmul_mx(
-                    out=y_ps[t][h][:],
-                    lhsT=w1w[:, 2 * P * t : 2 * P * (t + 1)].bitcast(FP4X4),
-                    lhsT_scale=w1s[:, P * t : P * (t + 1)],
-                    rhs=xw_p[h][:].bitcast(FP8X4),
-                    rhs_scale=xs_p[:, cols],
-                    start=True,
-                    stop=True,
-                )
+        def compare(cols, slots, k):
+            n = cols.stop - cols.start
+            label = "%d_%d_%d" % (cols.start, slots[0], k)
+            diff = ring.tile([P, len(slots), n], F32, name="diff")
+            tanh = tile("tanh" + label, [P, len(slots), n], F32)
+            for i, t in enumerate(slots):
+                neighbours = y_window[t][:].indirect(lists[k][:, cols.start // GROUP : cols.stop // GROUP])
+                nc.vector.tensor_tensor(diff[:, i, :], neighbours, y_own[t][:, cols], ALU.subtract)
+            nc.scalar.activation(out=tanh[:], in_=diff[:], func=ACT.Tanh, scale=2.0)
+            for i, t in enumerate(slots):
+                if k == 0:
+                    total = tile("one_term%d_%d" % (cols.start, t), [P, n], F32)[:]
+                    nc.scalar.activation(out=total, in_=tanh[:, i, :], func=ACT.Copy, scale=gain_quarter[:, t : t + 1])
+                elif k == 1:
+                    total = tile("two_terms%d_%d" % (cols.start, t), [P, n], F32)[:]
+                    nc.vector.scalar_tensor_tensor(total, tanh[:, i, :], gain_half[:, t : t + 1], partial[cols.start, t], ALU.mult, ALU.add)
+                else:
+                    total = z_slots[:, t, cols]
+                    nc.vector.scalar_tensor_tensor(total, tanh[:, i, :], gain[:, t : t + 1], partial[cols.start, t], ALU.mult, ALU.add)
+                partial[cols.start, t] = total
 
-        def fetch_y(t):
-            nc.scalar.copy(out=y_win[t][:, :HALF], in_=y_ps[t][0][:])
-            nc.scalar.copy(out=y_own[t][0][:], in_=y_ps[t][0][:])
-            nc.scalar.copy(out=y_win[t][:, HALF:], in_=y_ps[t][1][:])
-
-        def fetch_own(t):
-            nc.scalar.copy(out=y_own[t][1][:], in_=y_ps[t][1][:])
+        def census(cols, slots):
+            for k in range(3):
+                compare(cols, slots, k)
 
         zw = tile("zw", [P, S], U32)
         zs = tile("zs", [P, S], U8)
-        osc = tile("osc", [P, S], U8)
+        out_scales = tile("out_scales", [P, S], U8)
         out_rows = out_0.rearrange("(p t) j -> p t j", t=PACK)
         out_words = out_1[0].rearrange("p n t -> p (n t)").bitcast(I32)
+        out_ps = {}
+        early = slice(0, LAST * BLOCK)
+        early_bf16 = tile("early_bf16", [P, LAST * BLOCK, PACK], BF16)
+        first_f32 = tile("first_f32", [P, PACK, HALF], F32)
+        third_f32 = tile("third_f32", [P, PACK, BLOCK], F32)
 
-        z_rows = [tile("z_rows%d" % c, [P, PACK, n], BF16) for c, (lo, n) in enumerate(CHUNKS)]
-        partial = {}
-
-        def compare(c, ts, k):
-            lo, n = CHUNKS[c]
-            tag = "%d_%d_%d" % (c, ts[0], k)
-            diff = ring.tile([P, len(ts), n], F32, name="diff")
-            th = tile("th" + tag, [P, len(ts), n], F32)
-            for i, t in enumerate(ts):
-                nc.vector.tensor_tensor(
-                    diff[:, i, :],
-                    y_win[t][:].indirect(lists[k][:, lo // 16 : (lo + n) // 16]),
-                    y_own[t][lo // HALF][:, lo % HALF : lo % HALF + n],
-                    ALU.subtract,
-                )
-            nc.scalar.activation(out=th[:], in_=diff[:], func=ACT.Tanh, scale=2.0)
-            for i, t in enumerate(ts):
-                if k == 0:
-                    partial[c, t] = tile("first%d_%d" % (c, t), [P, n], F32)
-                    nc.scalar.activation(out=partial[c, t][:], in_=th[:, i, :], func=ACT.Copy, scale=gain_quarter[:, t : t + 1])
-                elif k == 1:
-                    second = tile("second%d_%d" % (c, t), [P, n], F32)
-                    nc.vector.scalar_tensor_tensor(second[:], th[:, i, :], gain_half[:, t : t + 1], partial[c, t][:], ALU.mult, ALU.add)
-                    partial[c, t] = second
-                else:
-                    nc.vector.scalar_tensor_tensor(z_rows[c][:, t, :], th[:, i, :], gain[:, t : t + 1], partial[c, t][:], ALU.mult, ALU.add)
-
-        def census(c, ts):
-            for k in range(3):
-                compare(c, ts, k)
-
-        o_ps = {}
-
-        def layer(b, copy):
-            cols = slice(b * BLOCK, (b + 1) * BLOCK)
-            c = [lo <= cols.start < lo + n for lo, n in CHUNKS].index(True)
-            lo = CHUNKS[c][0]
-            z16 = tile("z16_%d" % b, [P, BLOCK, PACK], BF16)
-            copy(out=z16[:], in_=z_rows[c][:, :, cols.start - lo : cols.stop - lo].rearrange("p t n -> p n t"))
-            nc.vector.quantize_mx(out=zw[:, cols].bitcast(FP8X4), scales=zs[:, cols], in_=z16[:].rearrange("p n t -> p (n t)"))
-            o_ps[b] = psum.tile([P, PACK, BLOCK], F32, name="o_ps%d" % b, tag="bank%d" % b)
+        def layer(b):
+            cols = block_columns(b)
+            z_interleaved = tile("z_interleaved%d" % b, [P, BLOCK, PACK], BF16)
+            nc.scalar.copy(out=z_interleaved[:], in_=z_slots[:, :, cols].rearrange("p t n -> p n t"))
+            quantise(nc, zw[:, cols], zs[:, cols], z_interleaved[:])
+            out_ps[b] = psum.tile([P, PACK, BLOCK], F32, name="out_ps%d" % b, tag="bank%d" % b)
             for t in range(PACK):
-                nc.tensor.matmul_mx(
-                    out=o_ps[b][:, t, :],
-                    lhsT=w2w[:, 2 * P * t : 2 * P * (t + 1)].bitcast(FP4X4),
-                    lhsT_scale=w2s[:, P * t : P * (t + 1)],
-                    rhs=zw[:, cols].bitcast(FP8X4),
-                    rhs_scale=zs[:, cols],
-                    start=True,
-                    stop=True,
-                )
+                product(nc, out_ps[b][:, t, :], w2w, w2s, t, zw[:, cols], zs[:, cols])
 
-        o16 = tile("o16", [P, S - BLOCK, PACK], BF16)
-
-        def round_result(b):
-            nc.scalar.copy(out=o16[:, b * BLOCK : (b + 1) * BLOCK, :], in_=o_ps[b][:].rearrange("p t n -> p n t"))
-
-        o32_chunk = [tile("o32_%d" % c, [P, PACK, n], F32) for c, (lo, n) in enumerate(CHUNKS[:2])]
-
-        def result(b):
-            c = b // 2
-            lo, n = CHUNKS[c]
-            nc.scalar.copy(out=o32_chunk[c][:, :, b * BLOCK - lo : (b + 1) * BLOCK - lo], in_=o_ps[b][:])
-            if (b + 1) * BLOCK == lo + n:
-                nc.sync.dma_start(out=out_rows[:, :, lo : lo + n], in_=o32_chunk[c][:])
-
-        def early_planes():
-            ow_early = keep.tile([P, S - BLOCK], U32, name="ow_early", tag="late", align_bytes=64)
-            for cols in (slice(0, 2 * BLOCK), slice(2 * BLOCK, 3 * BLOCK)):
-                nc.vector.quantize_mx(out=ow_early[:, cols].bitcast(FP8X4), scales=osc[:, cols], in_=o16[:, cols, :].rearrange("p n t -> p (n t)"))
-            nc.sync.dma_start(out=out_words[:, : S - BLOCK], in_=ow_early[:].bitcast(I32))
-
-        def last_block():
-            cols = slice(S - BLOCK, S)
-            z16 = keep.tile([P, BLOCK, PACK], BF16, name="z16_last", tag="late", align_bytes=64)
-            nc.vector.tensor_copy(out=z16[:], in_=z_rows[2][:].rearrange("p t n -> p n t"))
-            nc.vector.quantize_mx(out=zw[:, cols].bitcast(FP8X4), scales=zs[:, cols], in_=z16[:].rearrange("p n t -> p (n t)"))
-            pairs = [psum.tile([P, 2, BLOCK], F32, name="o_last%d" % u, tag="bank%d" % (3 + u)) for u in range(2)]
-            for t in range(PACK):
-                nc.tensor.matmul_mx(
-                    out=pairs[t // 2][:, t % 2, :],
-                    lhsT=w2w[:, 2 * P * t : 2 * P * (t + 1)].bitcast(FP4X4),
-                    lhsT_scale=w2s[:, P * t : P * (t + 1)],
-                    rhs=zw[:, cols].bitcast(FP8X4),
-                    rhs_scale=zs[:, cols],
-                    start=True,
-                    stop=True,
-                )
-            early_planes()
-            o32 = tile("o32_last", [P, PACK, BLOCK], F32)
-            nc.scalar.copy(out=o32[:, 0:2, :], in_=pairs[0][:])
-            nc.vector.tensor_copy(out=o32[:, 2:4, :], in_=pairs[1][:])
-            nc.scalar.dma_start(out=out_rows[:, :, cols], in_=o32[:])
-            o16_last = tile("o16_last", [P, BLOCK, PACK], BF16)
-            ow_last = tile("ow_last", [P, BLOCK], U32)
-            nc.vector.tensor_copy(out=o16_last[:], in_=o32[:].rearrange("p t n -> p n t"))
-            nc.vector.quantize_mx(out=ow_last[:].bitcast(FP8X4), scales=osc[:, cols], in_=o16_last[:].rearrange("p n t -> p (n t)"))
-            nc.sync.dma_start(out=out_words[:, cols], in_=ow_last[:].bitcast(I32))
-
-        fetch_y(0)
-        fetch_y(1)
+        fetch_window(0)
+        fetch_window(1)
         nc.scalar.activation(out=gain_quarter[:], in_=gain[:], func=ACT.Copy, scale=0.25)
         nc.scalar.activation(out=gain_half[:], in_=gain[:], func=ACT.Copy, scale=0.5)
-        census(0, [0])
-        fetch_y(2)
-        census(0, [1])
-        fetch_y(3)
-        fetch_own(0)
-        fetch_own(1)
-        census(0, [2])
-        fetch_own(2)
-        fetch_own(3)
-        census(0, [3])
-        layer(0, nc.scalar.copy)
-        layer(1, nc.scalar.copy)
-        census(1, [0, 1])
-        result(0)
-        result(1)
-        census(1, [2, 3])
-        layer(2, nc.scalar.copy)
-        census(2, [0, 1])
-        compare(2, [2, 3], 0)
-        compare(2, [2, 3], 1)
-        compare(2, [2], 2)
-        compare(2, [3], 2)
-        result(2)
-        round_result(0)
-        round_result(1)
-        round_result(2)
-        last_block()
-        for q in range(QUADS):
-            (nc.sync if q < 2 else nc.scalar).dma_start(out=out_2[0, 4 * q : 4 * q + 4, :].bitcast(I32), in_=osc[32 * q : 32 * q + 4, :].bitcast(I32))
+        for narrow, wide in zip(NARROW_SLOTS, WIDE_SLOTS):
+            census(slice(0, HALF), [narrow])
+            fetch_window(wide)
+            fetch_second_half(wide)
+        census(slice(0, S), WIDE_SLOTS[:1])
+        for narrow in NARROW_SLOTS:
+            fetch_second_half(narrow)
+        census(slice(0, S), WIDE_SLOTS[1:])
+
+        layer(0)
+        layer(1)
+        census(block_columns(2), NARROW_SLOTS)
+        layer(2)
+        last = block_columns(LAST)
+        compare(last, NARROW_SLOTS, 0)
+        compare(last, NARROW_SLOTS, 1)
+        for narrow in NARROW_SLOTS:
+            compare(last, [narrow], 2)
+
+        for b in range(2):
+            nc.scalar.copy(out=first_f32[:, :, block_columns(b)], in_=out_ps[b][:])
+        nc.sync.dma_start(out=out_rows[:, :, :HALF], in_=first_f32[:])
+        nc.scalar.copy(out=third_f32[:], in_=out_ps[2][:])
+        nc.sync.dma_start(out=out_rows[:, :, block_columns(2)], in_=third_f32[:])
+        for b in range(2):
+            nc.scalar.copy(out=early_bf16[:, block_columns(b), :], in_=out_ps[b][:].rearrange("p t n -> p n t"))
+
+        z_last = tile("z_last", [P, BLOCK, PACK], BF16, tag="z_last_then_early_words")
+        nc.vector.tensor_copy(out=z_last[:], in_=z_slots[:, :, last].rearrange("p t n -> p n t"))
+        quantise(nc, zw[:, last], zs[:, last], z_last[:])
+        last_ps = [psum.tile([P, 2, BLOCK], F32, name="last_ps%d" % u, tag="bank%d" % (LAST + u)) for u in range(2)]
+        for t in range(PACK):
+            product(nc, last_ps[t // 2][:, t % 2, :], w2w, w2s, t, zw[:, last], zs[:, last])
+
+        early_words = tile("early_words", [P, LAST * BLOCK], U32, tag="z_last_then_early_words")
+        nc.vector.tensor_copy(out=early_bf16[:, block_columns(2), :], in_=third_f32[:].rearrange("p t n -> p n t"))
+        for cols in (block_columns(2), slice(0, HALF)):
+            quantise(nc, early_words[:, cols], out_scales[:, cols], early_bf16[:, cols, :])
+        nc.sync.dma_start(out=out_words[:, early], in_=early_words[:].bitcast(I32))
+
+        last_f32 = tile("last_f32", [P, PACK, BLOCK], F32)
+        nc.scalar.copy(out=last_f32[:, 0:2, :], in_=last_ps[0][:])
+        nc.vector.tensor_copy(out=last_f32[:, 2:4, :], in_=last_ps[1][:])
+        nc.scalar.dma_start(out=out_rows[:, :, last], in_=last_f32[:])
+        last_bf16 = tile("last_bf16", [P, BLOCK, PACK], BF16)
+        last_words = tile("last_words", [P, BLOCK], U32)
+        nc.vector.tensor_copy(out=last_bf16[:], in_=last_f32[:].rearrange("p t n -> p n t"))
+        quantise(nc, last_words[:], out_scales[:, last], last_bf16[:])
+        nc.sync.dma_start(out=out_words[:, last], in_=last_words[:].bitcast(I32))
+
+        for q, queue in enumerate([nc.sync, nc.sync, nc.scalar, nc.scalar]):
+            queue.dma_start(out=out_2[0, 4 * q : 4 * q + 4, :].bitcast(I32), in_=out_scales[32 * q : 32 * q + 4, :].bitcast(I32))

from contextlib import ExitStack

import concourse.mybir as mybir

K, T, S, N, H = 512, 2048, 512, 512, 512
FLOPS = 2 * K * H * S + 2 * H * N * S

F32 = mybir.dt.float32
BF16 = mybir.dt.bfloat16
I32 = mybir.dt.int32
U32 = mybir.dt.uint32
U16 = mybir.dt.uint16
U8 = mybir.dt.uint8
FP8X4 = mybir.dt.float8_e4m3fn_x4
FP4X4 = mybir.dt.float4_e2m1fn_x4
ALU = mybir.AluOpType
ACT = mybir.ActivationFunctionType

P = 128
PACK = 4
QUADS = 4
GROUP = 16
HALF = S // 2
BLOCK = 128
LAST = S // BLOCK - 1
XS_CLEAR_SPLIT = 1152
DIFF_BUFS = 3
NARROW_SLOTS = [0, 1]
WIDE_SLOTS = [2, 3]


def load_scale_rows(queues, tile, scales):
    for q in range(QUADS):
        queues[q].dma_start(out=tile[32 * q : 32 * q + 4, :].bitcast(I32), in_=scales[0, 4 * q : 4 * q + 4, :].bitcast(I32))


def deal_words(nc, words, raw_words):
    nc.vector.tensor_copy(
        out=words[:].rearrange("p (t c m b) -> p c t m b", t=PACK, m=8, b=2),
        in_=raw_words[:].rearrange("p (c m t b) -> p c t m b", t=PACK, m=8, b=2),
    )


def deal_scales(nc, scales, raw_scales):
    nc.vector.tensor_copy(
        out=scales[:].rearrange("p (t c m) -> p c t m", t=PACK, m=16),
        in_=raw_scales[:].rearrange("p (c m t) -> p c t m", t=PACK, m=16),
    )


def product(nc, out, words, scales, t, moving_words, moving_scales):
    nc.tensor.matmul_mx(
        out=out,
        lhsT=words[:, 2 * P * t : 2 * P * (t + 1)].bitcast(FP4X4),
        lhsT_scale=scales[:, P * t : P * (t + 1)],
        rhs=moving_words.bitcast(FP8X4),
        rhs_scale=moving_scales,
        start=True,
        stop=True,
    )


def quantise(nc, words, scales, interleaved):
    nc.vector.quantize_mx(out=words.bitcast(FP8X4), scales=scales, in_=interleaved.rearrange("p n t -> p (n t)"))


def block_columns(b):
    return slice(b * BLOCK, (b + 1) * BLOCK)


def tile_picked_census8_none_po_kernel(
    tc, x_words, x_scales, w1_words, w1_scales, gn, w2_words, w2_scales, offs, p1, p2, p3, out_0, out_1, out_2
):
    nc = tc.nc
    with ExitStack() as ctx:
        keep = ctx.enter_context(tc.tile_pool(name="keep", bufs=1))
        ring = ctx.enter_context(tc.tile_pool(name="ring", bufs=DIFF_BUFS))
        psum = ctx.enter_context(tc.psum_pool(name="psum", bufs=1))

        def tile(name, shape, dtype, tag=None):
            return keep.tile(shape, dtype, name=name, tag=tag or name, align_bytes=64)

        offs_sb = tile("offs_sb", [P, S // GROUP], U16)
        lists = [tile("list%d" % k, [P, S // GROUP], U16) for k in range(3)]
        xw = tile("xw", [P, T], U32)
        xs = tile("xs", [P, T], U8)
        w1w_raw = tile("w1w_raw", [P, 2 * H], U8)
        w1s_raw = tile("w1s_raw", [P, H], U8, tag="w1_scales_then_picked_words")
        w2w_raw = tile("w2w_raw", [P, 2 * N], U8)
        w2s_raw = tile("w2s_raw", [P, N], U8)
        gain = tile("gain", [P, PACK], F32)

        nc.vector.memset(xs[:, :XS_CLEAR_SPLIT].bitcast(I32), 0)
        nc.gpsimd.memset(xs[:, XS_CLEAR_SPLIT:].bitcast(I32), 0)
        nc.vector.memset(w1s_raw[:].bitcast(I32), 0)
        nc.gpsimd.memset(w2s_raw[:].bitcast(I32), 0)

        nc.sync.dma_start(offs_sb[:], offs)
        nc.sync.dma_start(lists[0][:], p1)
        nc.sync.dma_start(out=w1w_raw[:].bitcast(I32), in_=w1_words[0].bitcast(I32))
        load_scale_rows([nc.scalar, nc.sync, nc.scalar, nc.sync], xs, x_scales)
        nc.sync.dma_start(out=xw[:].bitcast(I32), in_=x_words[0].rearrange("p n t -> p (n t)").bitcast(I32))
        load_scale_rows([nc.sync] * QUADS, w1s_raw, w1_scales)
        nc.sync.dma_start(lists[1][:], p2)
        nc.sync.dma_start(out=w2w_raw[:].bitcast(I32), in_=w2_words[0].bitcast(I32))
        nc.sync.dma_start(lists[2][:], p3)
        nc.sync.dma_start(out=gain[:], in_=gn.rearrange("(p t) o -> p (t o)", t=PACK))
        load_scale_rows([nc.sync] * QUADS, w2s_raw, w2_scales)

        xs_picked = tile("xs_picked", [P, S], U8)
        xw_picked = [tile("xw_picked0", [P, HALF], U32), tile("xw_picked1", [P, HALF], U32, tag="w1_scales_then_picked_words")]
        w1w = tile("w1w", [P, 2 * H], U8)
        w1s = tile("w1s", [P, H], U8)
        w2w = tile("w2w", [P, 2 * N], U8)
        w2s = tile("w2s", [P, N], U8)
        nc.vector.tensor_copy(out=xs_picked[:], in_=xs[:].indirect(offs_sb[:]))
        deal_words(nc, w1w, w1w_raw)
        deal_scales(nc, w1s, w1s_raw)
        for h in range(2):
            entries = offs_sb[:, h * HALF // GROUP : (h + 1) * HALF // GROUP]
            nc.vector.tensor_copy(out=xw_picked[h][:], in_=xw[:].indirect(entries))
        deal_words(nc, w2w, w2w_raw)
        deal_scales(nc, w2s, w2s_raw)

        y_ps = [[psum.tile([P, HALF], F32, name="y_ps%d_%d" % (t, h), tag="bank%d" % (2 * t + h)) for h in range(2)] for t in range(PACK)]
        y_window = [tile("y_window%d" % t, [P, 2 * S if t in WIDE_SLOTS else S], F32) for t in range(PACK)]
        y_own = [tile("y_own%d" % t, [P, S], F32) for t in range(PACK)]
        for t in WIDE_SLOTS:
            nc.vector.memset(y_window[t][:, S:], 0.0)
        for t in range(PACK):
            for h in range(2):
                product(nc, y_ps[t][h][:], w1w, w1s, t, xw_picked[h][:], xs_picked[:, h * HALF : (h + 1) * HALF])

        def fetch_window(t):
            nc.scalar.copy(out=y_window[t][:, :HALF], in_=y_ps[t][0][:])
            nc.scalar.copy(out=y_own[t][:, :HALF], in_=y_ps[t][0][:])
            nc.scalar.copy(out=y_window[t][:, HALF:S], in_=y_ps[t][1][:])

        def fetch_second_half(t):
            nc.scalar.copy(out=y_own[t][:, HALF:], in_=y_ps[t][1][:])

        gain_quarter = tile("gain_quarter", [P, PACK], F32)
        gain_half = tile("gain_half", [P, PACK], F32)
        z_slots = tile("z_slots", [P, PACK, S], BF16)
        partial = {}

        def compare(cols, slots, k):
            n = cols.stop - cols.start
            label = "%d_%d_%d" % (cols.start, slots[0], k)
            diff = ring.tile([P, len(slots), n], F32, name="diff")
            tanh = tile("tanh" + label, [P, len(slots), n], F32)
            for i, t in enumerate(slots):
                neighbours = y_window[t][:].indirect(lists[k][:, cols.start // GROUP : cols.stop // GROUP])
                nc.vector.tensor_tensor(diff[:, i, :], neighbours, y_own[t][:, cols], ALU.subtract)
            nc.scalar.activation(out=tanh[:], in_=diff[:], func=ACT.Tanh, scale=2.0)
            for i, t in enumerate(slots):
                if k == 0:
                    total = tile("one_term%d_%d" % (cols.start, t), [P, n], F32)[:]
                    nc.scalar.activation(out=total, in_=tanh[:, i, :], func=ACT.Copy, scale=gain_quarter[:, t : t + 1])
                elif k == 1:
                    total = tile("two_terms%d_%d" % (cols.start, t), [P, n], F32)[:]
                    nc.vector.scalar_tensor_tensor(total, tanh[:, i, :], gain_half[:, t : t + 1], partial[cols.start, t], ALU.mult, ALU.add)
                else:
                    total = z_slots[:, t, cols]
                    nc.vector.scalar_tensor_tensor(total, tanh[:, i, :], gain[:, t : t + 1], partial[cols.start, t], ALU.mult, ALU.add)
                partial[cols.start, t] = total

        def census(cols, slots):
            for k in range(3):
                compare(cols, slots, k)

        zw = tile("zw", [P, S], U32)
        zs = tile("zs", [P, S], U8)
        out_scales = tile("out_scales", [P, S], U8)
        out_rows = out_0.rearrange("(p t) j -> p t j", t=PACK)
        out_words = out_1[0].rearrange("p n t -> p (n t)").bitcast(I32)
        out_ps = {}
        early = slice(0, LAST * BLOCK)
        early_bf16 = tile("early_bf16", [P, LAST * BLOCK, PACK], BF16)
        first_f32 = tile("first_f32", [P, PACK, HALF], F32)
        third_f32 = tile("third_f32", [P, PACK, BLOCK], F32)

        def layer(b):
            cols = block_columns(b)
            z_interleaved = tile("z_interleaved%d" % b, [P, BLOCK, PACK], BF16)
            nc.scalar.copy(out=z_interleaved[:], in_=z_slots[:, :, cols].rearrange("p t n -> p n t"))
            quantise(nc, zw[:, cols], zs[:, cols], z_interleaved[:])
            out_ps[b] = psum.tile([P, PACK, BLOCK], F32, name="out_ps%d" % b, tag="bank%d" % b)
            for t in range(PACK):
                product(nc, out_ps[b][:, t, :], w2w, w2s, t, zw[:, cols], zs[:, cols])

        fetch_window(0)
        fetch_window(1)
        nc.scalar.activation(out=gain_quarter[:], in_=gain[:], func=ACT.Copy, scale=0.25)
        nc.scalar.activation(out=gain_half[:], in_=gain[:], func=ACT.Copy, scale=0.5)
        for narrow, wide in zip(NARROW_SLOTS, WIDE_SLOTS):
            census(slice(0, HALF), [narrow])
            fetch_window(wide)
            fetch_second_half(wide)
        census(slice(0, S), WIDE_SLOTS[:1])
        for narrow in NARROW_SLOTS:
            fetch_second_half(narrow)
        census(slice(0, S), WIDE_SLOTS[1:])

        layer(0)
        layer(1)
        census(block_columns(2), NARROW_SLOTS)
        layer(2)
        last = block_columns(LAST)
        compare(last, NARROW_SLOTS, 0)
        compare(last, NARROW_SLOTS, 1)
        for narrow in NARROW_SLOTS:
            compare(last, [narrow], 2)

        for b in range(2):
            nc.scalar.copy(out=first_f32[:, :, block_columns(b)], in_=out_ps[b][:])
        nc.sync.dma_start(out=out_rows[:, :, :HALF], in_=first_f32[:])
        nc.scalar.copy(out=third_f32[:], in_=out_ps[2][:])
        nc.sync.dma_start(out=out_rows[:, :, block_columns(2)], in_=third_f32[:])
        for b in range(2):
            nc.scalar.copy(out=early_bf16[:, block_columns(b), :], in_=out_ps[b][:].rearrange("p t n -> p n t"))

        z_last = tile("z_last", [P, BLOCK, PACK], BF16, tag="z_last_then_early_words")
        nc.vector.tensor_copy(out=z_last[:], in_=z_slots[:, :, last].rearrange("p t n -> p n t"))
        quantise(nc, zw[:, last], zs[:, last], z_last[:])
        last_ps = [psum.tile([P, 2, BLOCK], F32, name="last_ps%d" % u, tag="bank%d" % (LAST + u)) for u in range(2)]
        for t in range(PACK):
            product(nc, last_ps[t // 2][:, t % 2, :], w2w, w2s, t, zw[:, last], zs[:, last])

        early_words = tile("early_words", [P, LAST * BLOCK], U32, tag="z_last_then_early_words")
        nc.vector.tensor_copy(out=early_bf16[:, block_columns(2), :], in_=third_f32[:].rearrange("p t n -> p n t"))
        for cols in (block_columns(2), slice(0, HALF)):
            quantise(nc, early_words[:, cols], out_scales[:, cols], early_bf16[:, cols, :])
        nc.sync.dma_start(out=out_words[:, early], in_=early_words[:].bitcast(I32))

        last_f32 = tile("last_f32", [P, PACK, BLOCK], F32)
        nc.scalar.copy(out=last_f32[:, 0:2, :], in_=last_ps[0][:])
        nc.vector.tensor_copy(out=last_f32[:, 2:4, :], in_=last_ps[1][:])
        nc.scalar.dma_start(out=out_rows[:, :, last], in_=last_f32[:])
        last_bf16 = tile("last_bf16", [P, BLOCK, PACK], BF16)
        last_words = tile("last_words", [P, BLOCK], U32)
        nc.vector.tensor_copy(out=last_bf16[:], in_=last_f32[:].rearrange("p t n -> p n t"))
        quantise(nc, last_words[:], out_scales[:, last], last_bf16[:])
        nc.sync.dma_start(out=out_words[:, last], in_=last_words[:].bitcast(I32))

        for q, queue in enumerate([nc.sync, nc.sync, nc.scalar, nc.scalar]):
            queue.dma_start(out=out_2[0, 4 * q : 4 * q + 4, :].bitcast(I32), in_=out_scales[32 * q : 32 * q + 4, :].bitcast(I32))
